import numpy as np
import ml_dtypes


def mxq(x, axis, fmt="e4m3"):
    dtype, down = {"e4m3": (ml_dtypes.float8_e4m3fn, 7), "e5m2": (ml_dtypes.float8_e5m2, 14)}[fmt]
    v = np.moveaxis(np.asarray(x, np.float32).astype(ml_dtypes.bfloat16).astype(np.float64), axis, -1)
    blocks = v.reshape(v.shape[:-1] + (-1, 32))
    amax = np.abs(blocks).max(-1, keepdims=True)
    byte = np.maximum(np.where(amax > 0, np.frexp(amax)[1] - 1 + 127, 0) - down, 1)
    scale = np.exp2(byte - 127.0)
    codes = (blocks / scale).astype(np.float32).astype(dtype).astype(np.float64)
    return np.moveaxis((codes * scale).reshape(v.shape), -1, axis)


WIDE = False


def mx_kscale(k):
    if not WIDE:
        return np.ones(k)
    levels = np.array([10, -10, 5, -5, 0])
    if k % 512:
        return np.exp2(np.random.permutation(np.resize(levels, k // 32))).repeat(32)
    a = np.empty((k // 512, 16))
    for p in range(k // 512):
        a[p, :8] = np.random.permutation(np.resize(levels, 8))
        for g in range(8):
            far = levels[np.abs(levels - a[p, g]) >= 10]
            a[p, g + 8] = far[np.random.randint(len(far))]
    return np.exp2(a.ravel()).repeat(32)


def f64(x):
    return np.asarray(x).astype(np.float64)


def striped(idx):
    return np.tile(np.asarray(idx).reshape(-1, 16).T, (8, 1)).astype(np.uint16)


def unstriped(offs):
    return offs[:16].T.reshape(-1).astype(np.int64)


E2M1 = np.array([0.0, 0.5, 1.0, 1.5, 2.0, 3.0, 4.0, 6.0, -0.0, -0.5, -1.0, -1.5, -2.0, -3.0, -4.0, -6.0])


def pack_weight(w, fmt):
    k, n = w.shape
    w = f64(np.asarray(w, np.float32).astype(ml_dtypes.bfloat16)).reshape(k // 32, 32, n)
    amax = np.abs(w).max(1)
    if fmt == "e4m3":
        byte = np.frexp(amax)[1] - 1 + 127 - 7
    else:
        mant, ex = np.frexp(amax / 6.0)
        byte = np.where(mant > 0.5, ex, ex - 1) + 127
    byte = np.clip(np.where(amax > 0, byte, 1), 1, 254)
    scaled = (w * np.exp2(127.0 - byte)[:, None, :]).reshape(k, n).astype(np.float32)
    by_word = np.ascontiguousarray(scaled.reshape(k // 512, 128, 4, n).transpose(0, 1, 3, 2))
    if fmt == "e4m3":
        words = by_word.astype(ml_dtypes.float8_e4m3fn).view(np.uint8)
    else:
        c = by_word.astype(ml_dtypes.float4_e2m1fn).view(np.uint8) & 0xF
        words = (c[..., 0::2] | (c[..., 1::2] << 4)).reshape(k // 512, 128, 2 * n)
    return np.ascontiguousarray(words), np.ascontiguousarray(byte.astype(np.uint8).reshape(k // 512, 16, n))


def unpack_weight(words, scales, fmt):
    g, _, n = scales.shape
    words = np.ascontiguousarray(words).reshape(g, 128, n, -1)
    if fmt == "e4m3":
        vals = words.view(ml_dtypes.float8_e4m3fn).astype(np.float64)
    else:
        nib = np.empty((g, 128, n, 4), np.uint8)
        nib[..., 0::2] = words & 0xF
        nib[..., 1::2] = words >> 4
        vals = E2M1[nib]
    vals = vals * np.repeat(np.exp2(scales.astype(np.float64) - 127.0), 8, axis=1)[..., None]
    return vals.transpose(0, 1, 3, 2).reshape(g * 512, n)


D, K, R, T, I, Q, G = 512, 512, 512, 2048, 512, 128, 64


def setup_inputs():
    n = np.random.standard_normal
    idx = np.random.permutation(T)[:I]
    fd = mx_kscale(D)
    fk = mx_kscale(K)
    fr = mx_kscale(R)
    keysp = pack_weight(n((D, T)) / fd[:, None], "e2m1")
    tabp = pack_weight(n((K, T)) / fk[:, None], "e2m1")
    return {
        "query": (n((D, Q)) * 0.6 / np.sqrt(D) * fd[:, None]).astype(np.float32),
        "keys_words": keysp[0],
        "keys_scales": keysp[1],
        "sharp": (np.random.uniform(1.0, 3.0, (Q, 1))).astype(np.float32),
        "tab_words": tabp[0],
        "tab_scales": tabp[1],
        "w1": (n((K, R)) * 1 / np.sqrt(K) * fk[:, None]).astype(np.float32),
        "gain": (np.random.uniform(0.5, 2.0, (R, 1))).astype(np.float32),
        "gout": (n((R, Q)) * 1 / np.sqrt(R) * fr[:, None]).astype(np.float32),
        "hsc": (np.random.uniform(0.7, 1.4, (R, 1)) / fr[:, None]).astype(np.float32),
        "old": (0.5 * n((Q, T))).astype(np.float32),
        "offs": striped(idx),
    }


def reference(query, keys_words, keys_scales, sharp, tab_words, tab_scales, w1, gain, gout, hsc, old, offs):
    idx = unstriped(offs)
    keysu = unpack_weight(keys_words, keys_scales, "e2m1")
    tabu = unpack_weight(tab_words, tab_scales, "e2m1")
    queryq = mxq(f64(query), 0, "e4m3")
    keysidxg = keysu[:, idx]
    a = queryq.T @ keysidxg
    p = np.exp(a)
    s = p.reshape(Q, G, I // G).sum(axis=2)
    ms = a.reshape(Q, G, I // G).mean(axis=2) * f64(sharp)
    pg = np.exp(ms - np.max(ms, axis=1, keepdims=True))
    z = np.sum(pg, axis=1, keepdims=True)
    sh = pg / z / s
    rr = np.repeat(sh, I // G, axis=1)
    w1q = mxq(f64(w1), 0, "e4m3")
    tabidxg = tabu[:, idx]
    zh = w1q.T @ tabidxg
    ht = np.tanh(zh)
    hv = ht * f64(gain)
    hs1 = hv * f64(hsc)
    goutq = mxq(f64(gout), 0, "e4m3")
    hs1q = mxq(hs1, 0, "e4m3")
    c0 = goutq.T @ hs1q
    drr = c0 * p
    dsh = drr.reshape(Q, G, I // G).sum(axis=2)
    dz = np.sum(dsh / s * pg / np.square(z) * (-1.0), axis=1, keepdims=True)
    dpg = dsh / s / z + dz
    dms = dpg * pg
    e1 = dms * f64(sharp) / 8.0
    r1 = np.repeat(e1, I // G, axis=1)
    ds = dsh * pg / z / np.square(s) * (-1.0)
    r2 = np.repeat(ds, I // G, axis=1)
    dp = c0 * rr + r2
    da = r1 + dp * p
    gs = da * 512.0
    gf = np.zeros((Q, T))
    gf[:, idx] = gs
    y = f64(old) + gf
    return y

@@ -1,0 +1,212 @@
+from contextlib import ExitStack
+
+import concourse.mybir as mybir
+
+F32 = mybir.dt.float32
+BF16 = mybir.dt.bfloat16
+I32 = mybir.dt.int32
+U32 = mybir.dt.uint32
+U16 = mybir.dt.uint16
+U8 = mybir.dt.uint8
+FP8X4 = mybir.dt.float8_e4m3fn_x4
+FP4X4 = mybir.dt.float4_e2m1fn_x4
+ACT = mybir.ActivationFunctionType
+ALU = mybir.AluOpType
+AX = mybir.AxisListType
+
+P = 128
+PACK = 4
+R, T, SLOTS, Q, G = 512, 2048, 512, 128, 64
+GS = SLOTS // G
+CH = 128
+NCH = SLOTS // CH
+FLOPS = 402653184
+
+
+def tile_attend_blrgained_bygroup_kernel(
+    tc, query, keys_words, keys_scales, sharp, tab_words, tab_scales, w1, gain, gout, hsc, old, offs, out
+):
+    nc = tc.nc
+    with ExitStack() as ctx:
+        sb = ctx.enter_context(tc.tile_pool(name="sb", bufs=1))
+        ps = ctx.enter_context(tc.psum_pool(name="ps", bufs=1))
+
+        offsets = sb.tile([P, SLOTS // 16], U16, name="offsets")
+        kw = sb.tile([P, T], U16, name="kw")
+        ks = sb.tile([P, T], U8, name="ks")
+        tw = sb.tile([P, T], U16, name="tw")
+        tsc = sb.tile([P, T], U8, name="tsc")
+        window = sb.tile([P, T], F32, name="window")
+
+        nc.gpsimd.memset(ks[:].bitcast(I32), 0)
+        nc.vector.memset(tsc[:].bitcast(I32), 0)
+        nc.vector.memset(window[:], 0.0)
+
+        def load_scales(tile, rows):
+            for r in range(PACK):
+                nc.sync.dma_start(tile[r:P:32, :].bitcast(I32), rows[0, r:16:4, :].bitcast(I32))
+
+        sharp_sb = sb.tile([P, 1], F32, name="sharp_sb")
+        gain_sb = sb.tile([P, PACK], F32, name="gain_sb")
+        hsc_sb = sb.tile([P, PACK], F32, name="hsc_sb")
+
+        q_raw = sb.tile([P, PACK, Q], F32, name="q_raw")
+        g_raw = sb.tile([P, PACK, Q], F32, name="g_raw")
+        w_raw = [sb.tile([P, PACK, R // 2], F32, name=f"w_raw{h}", tag=f"w_raw{h}") for h in range(2)]
+        old_sb = sb.tile([P, T], F32, name="old_sb")
+
+        nc.sync.dma_start(offsets[:], offs)
+        nc.sync.dma_start(kw[:].bitcast(I32), keys_words[0].bitcast(I32))
+        load_scales(ks, keys_scales)
+        nc.sync.dma_start(q_raw[:], query.rearrange("(p j) q -> p j q", j=PACK))
+        nc.sync.dma_start(tw[:].bitcast(I32), tab_words[0].bitcast(I32))
+        w_view = w1.rearrange("(p j) r -> p j r", j=PACK)
+        for h in range(2):
+            nc.sync.dma_start(w_raw[h][:], w_view[:, :, h * (R // 2) : (h + 1) * (R // 2)])
+        load_scales(tsc, tab_scales)
+        nc.sync.dma_start(g_raw[:], gout.rearrange("(p j) q -> p j q", j=PACK))
+        nc.gpsimd.dma_start(sharp_sb[:], sharp)
+        nc.gpsimd.dma_start(gain_sb[:], gain.rearrange("(p t) o -> p (t o)", t=PACK))
+        nc.gpsimd.dma_start(hsc_sb[:], hsc.rearrange("(p t) o -> p (t o)", t=PACK))
+        nc.sync.dma_start(old_sb[:], old)
+
+        ns8 = sb.tile([P, 1], F32, name="ns8")
+        gh = sb.tile([P, PACK], F32, name="gh")
+        nc.gpsimd.tensor_tensor(gh[:], gain_sb[:], hsc_sb[:], ALU.mult)
+
+        def interleave(dst, src):
+            nc.scalar.copy(
+                dst[:].rearrange("p (c i) t -> p c t i", i=4),
+                src[:].rearrange("p t (c i) -> p c t i", i=4),
+            )
+
+        def quantize(codes, scales, src):
+            nc.vector.quantize_mx(out=codes.bitcast(FP8X4), scales=scales, in_=src)
+
+        q_bf = sb.tile([P, Q, PACK], BF16, name="q_bf", align_bytes=64)
+        interleave(q_bf, q_raw)
+        nc.scalar.activation(ns8[:], sharp_sb[:], ACT.Copy, scale=-1.0 / GS)
+        kwg = sb.tile([P, SLOTS], U16, name="kwg", align_bytes=64)
+        ksg = sb.tile([P, SLOTS], U8, name="ksg", align_bytes=64)
+        nc.vector.tensor_copy(kwg[:], kw[:].indirect(offsets[:]))
+        nc.vector.tensor_copy(ksg[:], ks[:].indirect(offsets[:]))
+        q_codes = sb.tile([P, Q], U32, name="q_codes", align_bytes=64)
+        q_scales = sb.tile([P, Q], U8, name="q_scales", align_bytes=64)
+        quantize(q_codes[:], q_scales[:], q_bf[:].rearrange("p q t -> p (q t)"))
+        a_ps = ps.tile([P, SLOTS], F32, name="a_ps")
+        nc.tensor.matmul_mx(
+            out=a_ps[:], lhsT=q_codes[:].bitcast(FP8X4), lhsT_scale=q_scales[:],
+            rhs=kwg[:].bitcast(FP4X4), rhs_scale=ksg[:], start=True, stop=True,
+        )
+        twg = sb.tile([P, SLOTS], U16, name="twg", align_bytes=64)
+        tsg = sb.tile([P, SLOTS], U8, name="tsg", align_bytes=64)
+        nc.vector.tensor_copy(twg[:], tw[:].indirect(offsets[:]))
+
+        p_sb = sb.tile([P, SLOTS], F32, name="p_sb")
+        nc.scalar.activation(p_sb[:], a_ps[:], ACT.Exp)
+        asum = sb.tile([P, G], F32, name="asum")
+        nc.vector.tensor_reduce(asum[:], a_ps[:].rearrange("p (g j) -> p g j", j=GS), AX.X, ALU.add)
+        nms = sb.tile([P, G], F32, name="nms")
+        negmax = sb.tile([P, 1], F32, name="negmax")
+        nc.vector.tensor_scalar(nms[:], asum[:], ns8[:], None, ALU.mult, ALU.min, accum_out=negmax[:])
+        sz = sb.tile([P, G + 1], F32, name="sz")
+        nc.vector.tensor_reduce(sz[:, :G], p_sb[:].rearrange("p (g j) -> p g j", j=GS), AX.X, ALU.add)
+        nc.vector.tensor_copy(tsg[:], tsc[:].indirect(offsets[:]))
+
+        w_bf = sb.tile([P, PACK, P, PACK], BF16, name="w_bf", align_bytes=64)
+        for h in range(2):
+            nc.scalar.copy(
+                w_bf[:, :, h * 64 : (h + 1) * 64, :].rearrange("p t m j -> p m j t"),
+                w_raw[h][:].rearrange("p j (m t) -> p m j t", t=PACK),
+            )
+        pg = sb.tile([P, G], F32, name="pg", tag="w_raw1")
+        nc.scalar.activation(pg[:], nms[:], ACT.Exp, bias=negmax[:], scale=-1.0, accum_out=sz[:, G : G + 1])
+        w_codes = sb.tile([P, R], U32, name="w_codes", align_bytes=64)
+        w_scales = sb.tile([P, R], U8, name="w_scales", align_bytes=64)
+        quantize(w_codes[:], w_scales[:], w_bf[:].rearrange("p t m j -> p (t m j)"))
+        rsz = sb.tile([P, G + 1], F32, name="rsz")
+        nc.vector.reciprocal(rsz[:], sz[:])
+
+        def by_group(ap):
+            return ap.rearrange("p (g j) -> p g j", j=GS)
+
+        def spread(ap, groups):
+            return ap.unsqueeze(2).to_broadcast([P, groups, GS])
+
+        n_sb = sb.tile([P, SLOTS], F32, name="n_sb")
+        nc.vector.scalar_tensor_tensor(
+            by_group(n_sb[:]), by_group(p_sb[:]), 512.0, spread(rsz[:, :G], G), ALU.mult, ALU.mult
+        )
+        g_bf = sb.tile([P, Q, PACK], BF16, name="g_bf", align_bytes=64)
+        interleave(g_bf, g_raw)
+        g_codes = sb.tile([P, Q], U32, name="g_codes", align_bytes=64)
+        g_scales = sb.tile([P, Q], U8, name="g_scales", align_bytes=64)
+        quantize(g_codes[:], g_scales[:], g_bf[:].rearrange("p q t -> p (q t)"))
+
+        zh = [ps.tile([P, PACK, CH], F32, name=f"zh{c}") for c in range(NCH)]
+        ht = [sb.tile([P, CH, PACK], F32, name=f"ht{c}") for c in range(NCH)]
+        hs = [sb.tile([P, CH, PACK], BF16, name=f"hs{c}", align_bytes=64) for c in range(NCH)]
+        h_codes = [sb.tile([P, CH], U32, name=f"h_codes{c}", align_bytes=64) for c in range(NCH)]
+        h_scales = [sb.tile([P, CH], U8, name=f"h_scales{c}", align_bytes=64) for c in range(NCH)]
+        FIRST = 3 * CH
+        c0a = ps.tile([P, FIRST], F32, name="c0a")
+        c0b = ps.tile([P, SLOTS - FIRST], F32, name="c0b")
+        c0 = [c0a[:, c * CH : (c + 1) * CH] for c in range(3)] + [c0b[:]]
+        for c in range(NCH):
+            cols = slice(c * CH, (c + 1) * CH)
+            for t in range(PACK):
+                m = slice(t * P, (t + 1) * P)
+                nc.tensor.matmul_mx(
+                    out=zh[c][:, t, :], lhsT=w_codes[:, m].bitcast(FP8X4), lhsT_scale=w_scales[:, m],
+                    rhs=twg[:, cols].bitcast(FP4X4), rhs_scale=tsg[:, cols], start=True, stop=True,
+                )
+            nc.scalar.activation(ht[c][:], zh[c][:].rearrange("p t n -> p n t"), ACT.Tanh)
+
+        na = sb.tile([P, SLOTS], F32, name="na")
+        nc.scalar.activation(na[:], n_sb[:], ACT.Identity, bias=ns8[:], scale=1.0 / 512.0)
+        wb = sb.tile([P, SLOTS], F32, name="wb")
+        nc.scalar.activation(by_group(wb[:]), spread(pg[:], G), ACT.Copy, scale=rsz[:, G : G + 1])
+
+        def scale_chunk(c):
+            nc.vector.tensor_tensor(hs[c][:], ht[c][:], gh[:].unsqueeze(1).to_broadcast([P, CH, PACK]), ALU.mult)
+
+        def product(c):
+            quantize(h_codes[c][:], h_scales[c][:], hs[c][:].rearrange("p n t -> p (n t)"))
+            nc.tensor.matmul_mx(
+                out=c0[c], lhsT=g_codes[:].bitcast(FP8X4), lhsT_scale=g_scales[:],
+                rhs=h_codes[c][:].bitcast(FP8X4), rhs_scale=h_scales[c][:], start=True, stop=True,
+            )
+
+        t_sb = sb.tile([P, SLOTS], F32, name="t_sb")
+        u = sb.tile([P, G], F32, name="u")
+        x_sb = sb.tile([P, SLOTS], F32, name="x_sb")
+        pa, pb = slice(0, FIRST), slice(FIRST, SLOTS)
+        ga, gb = slice(0, FIRST // GS), slice(FIRST // GS, G)
+
+        scale_chunk(0)
+        scale_chunk(1)
+        product(0)
+        scale_chunk(2)
+        product(1)
+        scale_chunk(3)
+        product(2)
+        product(3)
+        nc.vector.tensor_tensor(t_sb[:, pa], c0a[:], n_sb[:, pa], ALU.mult)
+        nc.vector.tensor_tensor(t_sb[:, pb], c0b[:], n_sb[:, pb], ALU.mult)
+        nc.vector.tensor_reduce(u[:, ga], by_group(t_sb[:, pa]), AX.X, ALU.add)
+        nc.vector.tensor_reduce(u[:, gb], by_group(t_sb[:, pb]), AX.X, ALU.add)
+        nc.vector.tensor_tensor(by_group(x_sb[:, pa]), by_group(na[:, pa]), spread(u[:, ga], FIRST // GS), ALU.mult)
+        uw = sb.tile([P, G], F32, name="uw")
+        negsm = sb.tile([P, 1], F32, name="negsm")
+        nc.vector.scalar_tensor_tensor(uw[:], u[:], ns8[:], wb[:, 0:SLOTS:GS], ALU.mult, ALU.mult, accum_out=negsm[:])
+        nc.vector.tensor_tensor(by_group(x_sb[:, pb]), by_group(na[:, pb]), spread(u[:, gb], G - FIRST // GS), ALU.mult)
+        y_sb = sb.tile([P, SLOTS], F32, name="y_sb")
+        nc.vector.scalar_tensor_tensor(y_sb[:], t_sb[:], negsm[:], x_sb[:], ALU.add, ALU.subtract)
+        nc.vector.tensor_tensor(window[:].indirect(offsets[:]), y_sb[:], wb[:], ALU.mult)
+
+        bounds = [0, 256, 768, 1280, 1792, 2048]
+        for k in range(len(bounds) - 1):
+            cols = slice(bounds[k], bounds[k + 1])
+            res = sb.tile([P, bounds[k + 1] - bounds[k]], F32, name=f"res{k}")
+            nc.vector.tensor_tensor(res[:], window[:, cols], old_sb[:, cols], ALU.add)
+            (nc.sync if k % 2 == 0 else nc.scalar).dma_start(out[:, cols], res[:])

@@ -33,13 +33,13 @@ def tile_attend_blrgained_bygroup_kernel(
 
         offsets = sb.tile([P, SLOTS // 16], U16, name="offsets")
         kw = sb.tile([P, T], U16, name="kw")
-        ks = sb.tile([P, T], U8, name="ks")
+        ks = sb.tile([P, T], U8, name="ks", tag="ks", align_bytes=64)
         tw = sb.tile([P, T], U16, name="tw")
-        tsc = sb.tile([P, T], U8, name="tsc")
+        tsc = sb.tile([P, T], U8, name="tsc", tag="tsc", align_bytes=64)
         window = sb.tile([P, T], F32, name="window")
 
         nc.gpsimd.memset(ks[:].bitcast(I32), 0)
-        nc.vector.memset(tsc[:].bitcast(I32), 0)
+        nc.gpsimd.memset(tsc[:].bitcast(I32), 0)
         nc.vector.memset(window[:], 0.0)
 
         def load_scales(tile, rows):
@@ -56,18 +56,18 @@ def tile_attend_blrgained_bygroup_kernel(
         old_sb = sb.tile([P, T], F32, name="old_sb")
 
         nc.sync.dma_start(offsets[:], offs)
-        nc.sync.dma_start(kw[:].bitcast(I32), keys_words[0].bitcast(I32))
         load_scales(ks, keys_scales)
+        nc.sync.dma_start(sharp_sb[:], sharp)
+        nc.sync.dma_start(kw[:].bitcast(I32), keys_words[0].bitcast(I32))
         nc.sync.dma_start(q_raw[:], query.rearrange("(p j) q -> p j q", j=PACK))
         nc.sync.dma_start(tw[:].bitcast(I32), tab_words[0].bitcast(I32))
         w_view = w1.rearrange("(p j) r -> p j r", j=PACK)
         for h in range(2):
             nc.sync.dma_start(w_raw[h][:], w_view[:, :, h * (R // 2) : (h + 1) * (R // 2)])
         load_scales(tsc, tab_scales)
+        nc.sync.dma_start(gain_sb[:], gain.rearrange("(p t) o -> p (t o)", t=PACK))
+        nc.sync.dma_start(hsc_sb[:], hsc.rearrange("(p t) o -> p (t o)", t=PACK))
         nc.sync.dma_start(g_raw[:], gout.rearrange("(p j) q -> p j q", j=PACK))
-        nc.gpsimd.dma_start(sharp_sb[:], sharp)
-        nc.gpsimd.dma_start(gain_sb[:], gain.rearrange("(p t) o -> p (t o)", t=PACK))
-        nc.gpsimd.dma_start(hsc_sb[:], hsc.rearrange("(p t) o -> p (t o)", t=PACK))
         nc.sync.dma_start(old_sb[:], old)
 
         ns8 = sb.tile([P, 1], F32, name="ns8")
@@ -83,13 +83,13 @@ def tile_attend_blrgained_bygroup_kernel(
         def quantize(codes, scales, src):
             nc.vector.quantize_mx(out=codes.bitcast(FP8X4), scales=scales, in_=src)
 
-        q_bf = sb.tile([P, Q, PACK], BF16, name="q_bf", align_bytes=64)
+        q_bf = sb.tile([P, Q, PACK], BF16, name="q_bf", tag="q_bf", align_bytes=64)
         interleave(q_bf, q_raw)
-        nc.scalar.activation(ns8[:], sharp_sb[:], ACT.Copy, scale=-1.0 / GS)
-        kwg = sb.tile([P, SLOTS], U16, name="kwg", align_bytes=64)
+        nc.gpsimd.tensor_scalar(ns8[:], sharp_sb[:], -1.0 / GS, 0.0, ALU.mult, ALU.add)
+        kwg = sb.tile([P, SLOTS], U16, name="kwg", tag="ks", align_bytes=64)
         ksg = sb.tile([P, SLOTS], U8, name="ksg", align_bytes=64)
-        nc.vector.tensor_copy(kwg[:], kw[:].indirect(offsets[:]))
         nc.vector.tensor_copy(ksg[:], ks[:].indirect(offsets[:]))
+        nc.vector.tensor_copy(kwg[:], kw[:].indirect(offsets[:]))
         q_codes = sb.tile([P, Q], U32, name="q_codes", align_bytes=64)
         q_scales = sb.tile([P, Q], U8, name="q_scales", align_bytes=64)
         quantize(q_codes[:], q_scales[:], q_bf[:].rearrange("p q t -> p (q t)"))
@@ -98,7 +98,7 @@ def tile_attend_blrgained_bygroup_kernel(
             out=a_ps[:], lhsT=q_codes[:].bitcast(FP8X4), lhsT_scale=q_scales[:],
             rhs=kwg[:].bitcast(FP4X4), rhs_scale=ksg[:], start=True, stop=True,
         )
-        twg = sb.tile([P, SLOTS], U16, name="twg", align_bytes=64)
+        twg = sb.tile([P, SLOTS], U16, name="twg", tag="q_bf", align_bytes=64)
         tsg = sb.tile([P, SLOTS], U8, name="tsg", align_bytes=64)
         nc.vector.tensor_copy(twg[:], tw[:].indirect(offsets[:]))
 
@@ -109,21 +109,21 @@ def tile_attend_blrgained_bygroup_kernel(
         nms = sb.tile([P, G], F32, name="nms")
         negmax = sb.tile([P, 1], F32, name="negmax")
         nc.vector.tensor_scalar(nms[:], asum[:], ns8[:], None, ALU.mult, ALU.min, accum_out=negmax[:])
-        sz = sb.tile([P, G + 1], F32, name="sz")
-        nc.vector.tensor_reduce(sz[:, :G], p_sb[:].rearrange("p (g j) -> p g j", j=GS), AX.X, ALU.add)
         nc.vector.tensor_copy(tsg[:], tsc[:].indirect(offsets[:]))
 
-        w_bf = sb.tile([P, PACK, P, PACK], BF16, name="w_bf", align_bytes=64)
+        w_bf = sb.tile([P, PACK, P, PACK], BF16, name="w_bf", tag="w_bf", align_bytes=64)
         for h in range(2):
             nc.scalar.copy(
                 w_bf[:, :, h * 64 : (h + 1) * 64, :].rearrange("p t m j -> p m j t"),
                 w_raw[h][:].rearrange("p j (m t) -> p m j t", t=PACK),
             )
-        pg = sb.tile([P, G], F32, name="pg", tag="w_raw1")
-        nc.scalar.activation(pg[:], nms[:], ACT.Exp, bias=negmax[:], scale=-1.0, accum_out=sz[:, G : G + 1])
-        w_codes = sb.tile([P, R], U32, name="w_codes", align_bytes=64)
+        w_codes = sb.tile([P, R], U32, name="w_codes", tag="tsc", align_bytes=64)
         w_scales = sb.tile([P, R], U8, name="w_scales", align_bytes=64)
         quantize(w_codes[:], w_scales[:], w_bf[:].rearrange("p t m j -> p (t m j)"))
+        sz = sb.tile([P, G + 1], F32, name="sz", tag="w_bf", align_bytes=64)
+        nc.vector.tensor_reduce(sz[:, :G], p_sb[:].rearrange("p (g j) -> p g j", j=GS), AX.X, ALU.add)
+        pg = sb.tile([P, G], F32, name="pg")
+        nc.scalar.activation(pg[:], nms[:], ACT.Exp, bias=negmax[:], scale=-1.0, accum_out=sz[:, G : G + 1])
         rsz = sb.tile([P, G + 1], F32, name="rsz")
         nc.vector.reciprocal(rsz[:], sz[:])
 
@@ -144,7 +144,7 @@ def tile_attend_blrgained_bygroup_kernel(
         quantize(g_codes[:], g_scales[:], g_bf[:].rearrange("p q t -> p (q t)"))
 
         zh = [ps.tile([P, PACK, CH], F32, name=f"zh{c}") for c in range(NCH)]
-        ht = [sb.tile([P, CH, PACK], F32, name=f"ht{c}") for c in range(NCH)]
+        ht = [sb.tile([P, CH, PACK], F32, name=f"ht{c}", tag=f"ht{c}") for c in range(NCH)]
         hs = [sb.tile([P, CH, PACK], BF16, name=f"hs{c}", align_bytes=64) for c in range(NCH)]
         h_codes = [sb.tile([P, CH], U32, name=f"h_codes{c}", align_bytes=64) for c in range(NCH)]
         h_scales = [sb.tile([P, CH], U8, name=f"h_scales{c}", align_bytes=64) for c in range(NCH)]
@@ -161,11 +161,6 @@ def tile_attend_blrgained_bygroup_kernel(
                     rhs=twg[:, cols].bitcast(FP4X4), rhs_scale=tsg[:, cols], start=True, stop=True,
                 )
             nc.scalar.activation(ht[c][:], zh[c][:].rearrange("p t n -> p n t"), ACT.Tanh)
-
-        na = sb.tile([P, SLOTS], F32, name="na")
-        nc.scalar.activation(na[:], n_sb[:], ACT.Identity, bias=ns8[:], scale=1.0 / 512.0)
-        wb = sb.tile([P, SLOTS], F32, name="wb")
-        nc.scalar.activation(by_group(wb[:]), spread(pg[:], G), ACT.Copy, scale=rsz[:, G : G + 1])
 
         def scale_chunk(c):
             nc.vector.tensor_tensor(hs[c][:], ht[c][:], gh[:].unsqueeze(1).to_broadcast([P, CH, PACK]), ALU.mult)
@@ -185,6 +180,11 @@ def tile_attend_blrgained_bygroup_kernel(
 
         scale_chunk(0)
         scale_chunk(1)
+        na = sb.tile([P, SLOTS], F32, name="na", tag="ht1")
+        nc.scalar.activation(na[:], n_sb[:], ACT.Identity, bias=ns8[:], scale=1.0 / 512.0)
+        wb = sb.tile([P, SLOTS], F32, name="wb", tag="ht0")
+        nc.scalar.activation(by_group(wb[:]), spread(pg[:], G), ACT.Copy, scale=rsz[:, G : G + 1])
+
         product(0)
         scale_chunk(2)
         product(1)

@@ -33,7 +33,7 @@ def tile_attend_blrgained_bygroup_kernel(
 
         offsets = sb.tile([P, SLOTS // 16], U16, name="offsets")
         kw = sb.tile([P, T], U16, name="kw")
-        ks = sb.tile([P, T], U8, name="ks", tag="ks", align_bytes=64)
+        ks = sb.tile([P, T], U8, name="ks")
         tw = sb.tile([P, T], U16, name="tw")
         tsc = sb.tile([P, T], U8, name="tsc", tag="tsc", align_bytes=64)
         window = sb.tile([P, T], F32, name="window")
@@ -55,12 +55,12 @@ def tile_attend_blrgained_bygroup_kernel(
         w_raw = [sb.tile([P, PACK, R // 2], F32, name=f"w_raw{h}", tag=f"w_raw{h}") for h in range(2)]
         old_sb = sb.tile([P, T], F32, name="old_sb")
 
-        nc.sync.dma_start(offsets[:], offs)
-        load_scales(ks, keys_scales)
-        nc.sync.dma_start(sharp_sb[:], sharp)
         nc.sync.dma_start(kw[:].bitcast(I32), keys_words[0].bitcast(I32))
+        nc.sync.dma_start(offsets[:], offs)
         nc.sync.dma_start(q_raw[:], query.rearrange("(p j) q -> p j q", j=PACK))
+        load_scales(ks, keys_scales)
         nc.sync.dma_start(tw[:].bitcast(I32), tab_words[0].bitcast(I32))
+        nc.sync.dma_start(sharp_sb[:], sharp)
         w_view = w1.rearrange("(p j) r -> p j r", j=PACK)
         for h in range(2):
             nc.sync.dma_start(w_raw[h][:], w_view[:, :, h * (R // 2) : (h + 1) * (R // 2)])
@@ -76,20 +76,20 @@ def tile_attend_blrgained_bygroup_kernel(
 
         def interleave(dst, src):
             nc.scalar.copy(
-                dst[:].rearrange("p (c i) t -> p c t i", i=4),
-                src[:].rearrange("p t (c i) -> p c t i", i=4),
+                dst.rearrange("p (c i) t -> p c t i", i=4),
+                src.rearrange("p t (c i) -> p c t i", i=4),
             )
 
         def quantize(codes, scales, src):
             nc.vector.quantize_mx(out=codes.bitcast(FP8X4), scales=scales, in_=src)
 
         q_bf = sb.tile([P, Q, PACK], BF16, name="q_bf", tag="q_bf", align_bytes=64)
-        interleave(q_bf, q_raw)
+        interleave(q_bf[:], q_raw[:])
         nc.gpsimd.tensor_scalar(ns8[:], sharp_sb[:], -1.0 / GS, 0.0, ALU.mult, ALU.add)
-        kwg = sb.tile([P, SLOTS], U16, name="kwg", tag="ks", align_bytes=64)
+        kwg = sb.tile([P, SLOTS], U16, name="kwg", align_bytes=64)
         ksg = sb.tile([P, SLOTS], U8, name="ksg", align_bytes=64)
-        nc.vector.tensor_copy(ksg[:], ks[:].indirect(offsets[:]))
         nc.vector.tensor_copy(kwg[:], kw[:].indirect(offsets[:]))
+        nc.vector.tensor_copy(ksg[:], ks[:].indirect(offsets[:]))
         q_codes = sb.tile([P, Q], U32, name="q_codes", align_bytes=64)
         q_scales = sb.tile([P, Q], U8, name="q_scales", align_bytes=64)
         quantize(q_codes[:], q_scales[:], q_bf[:].rearrange("p q t -> p (q t)"))
@@ -102,14 +102,12 @@ def tile_attend_blrgained_bygroup_kernel(
         tsg = sb.tile([P, SLOTS], U8, name="tsg", align_bytes=64)
         nc.vector.tensor_copy(twg[:], tw[:].indirect(offsets[:]))
 
-        p_sb = sb.tile([P, SLOTS], F32, name="p_sb")
-        nc.scalar.activation(p_sb[:], a_ps[:], ACT.Exp)
-        asum = sb.tile([P, G], F32, name="asum")
+        asum = sb.tile([P, G], F32, name="asum", tag="asum", align_bytes=64)
         nc.vector.tensor_reduce(asum[:], a_ps[:].rearrange("p (g j) -> p g j", j=GS), AX.X, ALU.add)
-        nms = sb.tile([P, G], F32, name="nms")
+        nc.vector.tensor_copy(tsg[:], tsc[:].indirect(offsets[:]))
+        nms = sb.tile([P, G], F32, name="nms", tag="tsc", align_bytes=64)
         negmax = sb.tile([P, 1], F32, name="negmax")
         nc.vector.tensor_scalar(nms[:], asum[:], ns8[:], None, ALU.mult, ALU.min, accum_out=negmax[:])
-        nc.vector.tensor_copy(tsg[:], tsc[:].indirect(offsets[:]))
 
         w_bf = sb.tile([P, PACK, P, PACK], BF16, name="w_bf", tag="w_bf", align_bytes=64)
         for h in range(2):
@@ -117,7 +115,9 @@ def tile_attend_blrgained_bygroup_kernel(
                 w_bf[:, :, h * 64 : (h + 1) * 64, :].rearrange("p t m j -> p m j t"),
                 w_raw[h][:].rearrange("p j (m t) -> p m j t", t=PACK),
             )
-        w_codes = sb.tile([P, R], U32, name="w_codes", tag="tsc", align_bytes=64)
+        p_sb = sb.tile([P, SLOTS], F32, name="p_sb", tag="w_raw1")
+        nc.scalar.activation(p_sb[:], a_ps[:], ACT.Exp)
+        w_codes = sb.tile([P, R], U32, name="w_codes", tag="asum", align_bytes=64)
         w_scales = sb.tile([P, R], U8, name="w_scales", align_bytes=64)
         quantize(w_codes[:], w_scales[:], w_bf[:].rearrange("p t m j -> p (t m j)"))
         sz = sb.tile([P, G + 1], F32, name="sz", tag="w_bf", align_bytes=64)
@@ -133,21 +133,13 @@ def tile_attend_blrgained_bygroup_kernel(
         def spread(ap, groups):
             return ap.unsqueeze(2).to_broadcast([P, groups, GS])
 
-        n_sb = sb.tile([P, SLOTS], F32, name="n_sb")
-        nc.vector.scalar_tensor_tensor(
-            by_group(n_sb[:]), by_group(p_sb[:]), 512.0, spread(rsz[:, :G], G), ALU.mult, ALU.mult
-        )
-        g_bf = sb.tile([P, Q, PACK], BF16, name="g_bf", align_bytes=64)
-        interleave(g_bf, g_raw)
-        g_codes = sb.tile([P, Q], U32, name="g_codes", align_bytes=64)
-        g_scales = sb.tile([P, Q], U8, name="g_scales", align_bytes=64)
-        quantize(g_codes[:], g_scales[:], g_bf[:].rearrange("p q t -> p (q t)"))
-
         zh = [ps.tile([P, PACK, CH], F32, name=f"zh{c}") for c in range(NCH)]
         ht = [sb.tile([P, CH, PACK], F32, name=f"ht{c}", tag=f"ht{c}") for c in range(NCH)]
-        hs = [sb.tile([P, CH, PACK], BF16, name=f"hs{c}", align_bytes=64) for c in range(NCH)]
-        h_codes = [sb.tile([P, CH], U32, name=f"h_codes{c}", align_bytes=64) for c in range(NCH)]
-        h_scales = [sb.tile([P, CH], U8, name=f"h_scales{c}", align_bytes=64) for c in range(NCH)]
+        wide = [CH + Q] + [CH] * (NCH - 1)
+        hs = [sb.tile([P, wide[c], PACK], BF16, name=f"hs{c}", align_bytes=64) for c in range(NCH)]
+        h_codes = [sb.tile([P, wide[c]], U32, name=f"h_codes{c}", align_bytes=64) for c in range(NCH)]
+        h_scales = [sb.tile([P, wide[c]], U8, name=f"h_scales{c}", align_bytes=64) for c in range(NCH)]
+        interleave(hs[0][:, CH:, :], g_raw[:])
         FIRST = 3 * CH
         c0a = ps.tile([P, FIRST], F32, name="c0a")
         c0b = ps.tile([P, SLOTS - FIRST], F32, name="c0b")
@@ -163,13 +155,13 @@ def tile_attend_blrgained_bygroup_kernel(
             nc.scalar.activation(ht[c][:], zh[c][:].rearrange("p t n -> p n t"), ACT.Tanh)
 
         def scale_chunk(c):
-            nc.vector.tensor_tensor(hs[c][:], ht[c][:], gh[:].unsqueeze(1).to_broadcast([P, CH, PACK]), ALU.mult)
+            nc.vector.tensor_tensor(hs[c][:, :CH, :], ht[c][:], gh[:].unsqueeze(1).to_broadcast([P, CH, PACK]), ALU.mult)
 
         def product(c):
             quantize(h_codes[c][:], h_scales[c][:], hs[c][:].rearrange("p n t -> p (n t)"))
             nc.tensor.matmul_mx(
-                out=c0[c], lhsT=g_codes[:].bitcast(FP8X4), lhsT_scale=g_scales[:],
-                rhs=h_codes[c][:].bitcast(FP8X4), rhs_scale=h_scales[c][:], start=True, stop=True,
+                out=c0[c], lhsT=h_codes[0][:, CH:].bitcast(FP8X4), lhsT_scale=h_scales[0][:, CH:],
+                rhs=h_codes[c][:, :CH].bitcast(FP8X4), rhs_scale=h_scales[c][:, :CH], start=True, stop=True,
             )
 
         t_sb = sb.tile([P, SLOTS], F32, name="t_sb")
@@ -179,6 +171,10 @@ def tile_attend_blrgained_bygroup_kernel(
         ga, gb = slice(0, FIRST // GS), slice(FIRST // GS, G)
 
         scale_chunk(0)
+        n_sb = sb.tile([P, SLOTS], F32, name="n_sb")
+        nc.vector.scalar_tensor_tensor(
+            by_group(n_sb[:]), by_group(p_sb[:]), 512.0, spread(rsz[:, :G], G), ALU.mult, ALU.mult
+        )
         scale_chunk(1)
         na = sb.tile([P, SLOTS], F32, name="na", tag="ht1")
         nc.scalar.activation(na[:], n_sb[:], ACT.Identity, bias=ns8[:], scale=1.0 / 512.0)

@@ -34,12 +34,12 @@ def tile_attend_blrgained_bygroup_kernel(
         offsets = sb.tile([P, SLOTS // 16], U16, name="offsets")
         kw = sb.tile([P, T], U16, name="kw")
         ks = sb.tile([P, T], U8, name="ks")
-        tw = sb.tile([P, T], U16, name="tw")
+        tw = sb.tile([P, T], U16, name="tw", tag="tw")
         tsc = sb.tile([P, T], U8, name="tsc", tag="tsc", align_bytes=64)
         window = sb.tile([P, T], F32, name="window")
 
-        nc.gpsimd.memset(ks[:].bitcast(I32), 0)
-        nc.gpsimd.memset(tsc[:].bitcast(I32), 0)
+        nc.vector.memset(ks[:].bitcast(I32), 0)
+        nc.vector.memset(tsc[:].bitcast(I32), 0)
         nc.vector.memset(window[:], 0.0)
 
         def load_scales(tile, rows):
@@ -60,10 +60,10 @@ def tile_attend_blrgained_bygroup_kernel(
         nc.sync.dma_start(q_raw[:], query.rearrange("(p j) q -> p j q", j=PACK))
         load_scales(ks, keys_scales)
         nc.sync.dma_start(tw[:].bitcast(I32), tab_words[0].bitcast(I32))
-        nc.sync.dma_start(sharp_sb[:], sharp)
         w_view = w1.rearrange("(p j) r -> p j r", j=PACK)
         for h in range(2):
             nc.sync.dma_start(w_raw[h][:], w_view[:, :, h * (R // 2) : (h + 1) * (R // 2)])
+        nc.sync.dma_start(sharp_sb[:], sharp)
         load_scales(tsc, tab_scales)
         nc.sync.dma_start(gain_sb[:], gain.rearrange("(p t) o -> p (t o)", t=PACK))
         nc.sync.dma_start(hsc_sb[:], hsc.rearrange("(p t) o -> p (t o)", t=PACK))
@@ -102,12 +102,9 @@ def tile_attend_blrgained_bygroup_kernel(
         tsg = sb.tile([P, SLOTS], U8, name="tsg", align_bytes=64)
         nc.vector.tensor_copy(twg[:], tw[:].indirect(offsets[:]))
 
-        asum = sb.tile([P, G], F32, name="asum", tag="asum", align_bytes=64)
+        asum = sb.tile([P, G], F32, name="asum", tag="tw")
         nc.vector.tensor_reduce(asum[:], a_ps[:].rearrange("p (g j) -> p g j", j=GS), AX.X, ALU.add)
         nc.vector.tensor_copy(tsg[:], tsc[:].indirect(offsets[:]))
-        nms = sb.tile([P, G], F32, name="nms", tag="tsc", align_bytes=64)
-        negmax = sb.tile([P, 1], F32, name="negmax")
-        nc.vector.tensor_scalar(nms[:], asum[:], ns8[:], None, ALU.mult, ALU.min, accum_out=negmax[:])
 
         w_bf = sb.tile([P, PACK, P, PACK], BF16, name="w_bf", tag="w_bf", align_bytes=64)
         for h in range(2):
@@ -117,15 +114,19 @@ def tile_attend_blrgained_bygroup_kernel(
             )
         p_sb = sb.tile([P, SLOTS], F32, name="p_sb", tag="w_raw1")
         nc.scalar.activation(p_sb[:], a_ps[:], ACT.Exp)
-        w_codes = sb.tile([P, R], U32, name="w_codes", tag="asum", align_bytes=64)
+        w_codes = sb.tile([P, R], U32, name="w_codes", tag="tsc", align_bytes=64)
         w_scales = sb.tile([P, R], U8, name="w_scales", align_bytes=64)
         quantize(w_codes[:], w_scales[:], w_bf[:].rearrange("p t m j -> p (t m j)"))
-        sz = sb.tile([P, G + 1], F32, name="sz", tag="w_bf", align_bytes=64)
-        nc.vector.tensor_reduce(sz[:, :G], p_sb[:].rearrange("p (g j) -> p g j", j=GS), AX.X, ALU.add)
+        stats = sb.tile([P, 2, G], F32, name="stats", tag="w_bf", align_bytes=64)
+        s_sum, nms = stats[:, 0, :], stats[:, 1, :]
+        nc.vector.tensor_reduce(s_sum, p_sb[:].rearrange("p (g j) -> p g j", j=GS), AX.X, ALU.add)
+        negmax = sb.tile([P, 1], F32, name="negmax")
+        nc.vector.tensor_scalar(nms, asum[:], ns8[:], None, ALU.mult, ALU.min, accum_out=negmax[:])
+        rs = sb.tile([P, G], F32, name="rs")
+        nc.vector.reciprocal(rs[:], s_sum)
         pg = sb.tile([P, G], F32, name="pg")
-        nc.scalar.activation(pg[:], nms[:], ACT.Exp, bias=negmax[:], scale=-1.0, accum_out=sz[:, G : G + 1])
-        rsz = sb.tile([P, G + 1], F32, name="rsz")
-        nc.vector.reciprocal(rsz[:], sz[:])
+        z = sb.tile([P, 1], F32, name="z")
+        nc.scalar.activation(pg[:], nms, ACT.Exp, bias=negmax[:], scale=-1.0, accum_out=z[:])
 
         def by_group(ap):
             return ap.rearrange("p (g j) -> p g j", j=GS)
@@ -173,13 +174,15 @@ def tile_attend_blrgained_bygroup_kernel(
         scale_chunk(0)
         n_sb = sb.tile([P, SLOTS], F32, name="n_sb")
         nc.vector.scalar_tensor_tensor(
-            by_group(n_sb[:]), by_group(p_sb[:]), 512.0, spread(rsz[:, :G], G), ALU.mult, ALU.mult
+            by_group(n_sb[:]), by_group(p_sb[:]), 512.0, spread(rs[:], G), ALU.mult, ALU.mult
         )
+        rz = sb.tile([P, 1], F32, name="rz")
+        nc.vector.reciprocal(rz[:], z[:])
         scale_chunk(1)
         na = sb.tile([P, SLOTS], F32, name="na", tag="ht1")
         nc.scalar.activation(na[:], n_sb[:], ACT.Identity, bias=ns8[:], scale=1.0 / 512.0)
         wb = sb.tile([P, SLOTS], F32, name="wb", tag="ht0")
-        nc.scalar.activation(by_group(wb[:]), spread(pg[:], G), ACT.Copy, scale=rsz[:, G : G + 1])
+        nc.scalar.activation(by_group(wb[:]), spread(pg[:], G), ACT.Copy, scale=rz[:])
 
         product(0)
         scale_chunk(2)

@@ -35,7 +35,7 @@ def tile_attend_blrgained_bygroup_kernel(
         kw = sb.tile([P, T], U16, name="kw")
         ks = sb.tile([P, T], U8, name="ks")
         tw = sb.tile([P, T], U16, name="tw", tag="tw")
-        tsc = sb.tile([P, T], U8, name="tsc", tag="tsc", align_bytes=64)
+        tsc = sb.tile([P, T], U8, name="tsc")
         window = sb.tile([P, T], F32, name="window")
 
         nc.vector.memset(ks[:].bitcast(I32), 0)
@@ -61,10 +61,10 @@ def tile_attend_blrgained_bygroup_kernel(
         load_scales(ks, keys_scales)
         nc.sync.dma_start(tw[:].bitcast(I32), tab_words[0].bitcast(I32))
         w_view = w1.rearrange("(p j) r -> p j r", j=PACK)
-        for h in range(2):
-            nc.sync.dma_start(w_raw[h][:], w_view[:, :, h * (R // 2) : (h + 1) * (R // 2)])
-        nc.sync.dma_start(sharp_sb[:], sharp)
+        nc.sync.dma_start(w_raw[0][:], w_view[:, :, : R // 2])
         load_scales(tsc, tab_scales)
+        nc.sync.dma_start(w_raw[1][:], w_view[:, :, R // 2 :])
+        nc.sync.dma_start(sharp_sb[:], sharp)
         nc.sync.dma_start(gain_sb[:], gain.rearrange("(p t) o -> p (t o)", t=PACK))
         nc.sync.dma_start(hsc_sb[:], hsc.rearrange("(p t) o -> p (t o)", t=PACK))
         nc.sync.dma_start(g_raw[:], gout.rearrange("(p j) q -> p j q", j=PACK))
@@ -107,14 +107,18 @@ def tile_attend_blrgained_bygroup_kernel(
         nc.vector.tensor_copy(tsg[:], tsc[:].indirect(offsets[:]))
 
         w_bf = sb.tile([P, PACK, P, PACK], BF16, name="w_bf", tag="w_bf", align_bytes=64)
-        for h in range(2):
-            nc.scalar.copy(
-                w_bf[:, :, h * 64 : (h + 1) * 64, :].rearrange("p t m j -> p m j t"),
-                w_raw[h][:].rearrange("p j (m t) -> p m j t", t=PACK),
+        def deal(copy, h, m0, m1):
+            copy(
+                w_bf[:, :, h * 64 + m0 : h * 64 + m1, :].rearrange("p t m j -> p m j t"),
+                w_raw[h][:, :, PACK * m0 : PACK * m1].rearrange("p j (m t) -> p m j t", t=PACK),
             )
+
+        deal(nc.scalar.copy, 0, 0, 64)
+        deal(nc.scalar.copy, 1, 0, 32)
+        deal(nc.vector.tensor_copy, 1, 32, 64)
         p_sb = sb.tile([P, SLOTS], F32, name="p_sb", tag="w_raw1")
         nc.scalar.activation(p_sb[:], a_ps[:], ACT.Exp)
-        w_codes = sb.tile([P, R], U32, name="w_codes", tag="tsc", align_bytes=64)
+        w_codes = sb.tile([P, R], U32, name="w_codes", align_bytes=64)
         w_scales = sb.tile([P, R], U8, name="w_scales", align_bytes=64)
         quantize(w_codes[:], w_scales[:], w_bf[:].rearrange("p t m j -> p (t m j)"))
         stats = sb.tile([P, 2, G], F32, name="stats", tag="w_bf", align_bytes=64)

from contextlib import ExitStack

import concourse.mybir as mybir

F32 = mybir.dt.float32
BF16 = mybir.dt.bfloat16
I32 = mybir.dt.int32
U32 = mybir.dt.uint32
U16 = mybir.dt.uint16
U8 = mybir.dt.uint8
FP8X4 = mybir.dt.float8_e4m3fn_x4
FP4X4 = mybir.dt.float4_e2m1fn_x4
ACT = mybir.ActivationFunctionType
ALU = mybir.AluOpType
AX = mybir.AxisListType

P = 128
PACK = 4
R, T, SLOTS, Q, G = 512, 2048, 512, 128, 64
GS = SLOTS // G
CH = 128
NCH = SLOTS // CH
FLOPS = 402653184


def tile_attend_blrgained_bygroup_kernel(
    tc, query, keys_words, keys_scales, sharp, tab_words, tab_scales, w1, gain, gout, hsc, old, offs, out
):
    nc = tc.nc
    with ExitStack() as ctx:
        sb = ctx.enter_context(tc.tile_pool(name="sb", bufs=1))
        ps = ctx.enter_context(tc.psum_pool(name="ps", bufs=1))

        offsets = sb.tile([P, SLOTS // 16], U16, name="offsets")
        kw = sb.tile([P, T], U16, name="kw")
        ks = sb.tile([P, T], U8, name="ks")
        tw = sb.tile([P, T], U16, name="tw", tag="tw")
        tsc = sb.tile([P, T], U8, name="tsc")
        window = sb.tile([P, T], F32, name="window")

        nc.vector.memset(ks[:].bitcast(I32), 0)
        nc.vector.memset(tsc[:].bitcast(I32), 0)
        nc.vector.memset(window[:], 0.0)

        def load_scales(tile, rows):
            for r in range(PACK):
                nc.sync.dma_start(tile[r:P:32, :].bitcast(I32), rows[0, r:16:4, :].bitcast(I32))

        sharp_sb = sb.tile([P, 1], F32, name="sharp_sb")
        gain_sb = sb.tile([P, PACK], F32, name="gain_sb")
        hsc_sb = sb.tile([P, PACK], F32, name="hsc_sb")

        q_raw = sb.tile([P, PACK, Q], F32, name="q_raw")
        g_raw = sb.tile([P, PACK, Q], F32, name="g_raw")
        w_raw = [sb.tile([P, PACK, R // 2], F32, name=f"w_raw{h}", tag=f"w_raw{h}") for h in range(2)]
        old_sb = sb.tile([P, T], F32, name="old_sb")

        nc.sync.dma_start(kw[:].bitcast(I32), keys_words[0].bitcast(I32))
        nc.sync.dma_start(offsets[:], offs)
        nc.sync.dma_start(q_raw[:], query.rearrange("(p j) q -> p j q", j=PACK))
        load_scales(ks, keys_scales)
        nc.sync.dma_start(tw[:].bitcast(I32), tab_words[0].bitcast(I32))
        w_view = w1.rearrange("(p j) r -> p j r", j=PACK)
        nc.sync.dma_start(w_raw[0][:], w_view[:, :, : R // 2])
        load_scales(tsc, tab_scales)
        nc.sync.dma_start(w_raw[1][:], w_view[:, :, R // 2 :])
        nc.sync.dma_start(sharp_sb[:], sharp)
        nc.sync.dma_start(gain_sb[:], gain.rearrange("(p t) o -> p (t o)", t=PACK))
        nc.sync.dma_start(hsc_sb[:], hsc.rearrange("(p t) o -> p (t o)", t=PACK))
        nc.sync.dma_start(g_raw[:], gout.rearrange("(p j) q -> p j q", j=PACK))
        nc.sync.dma_start(old_sb[:], old)

        ns8 = sb.tile([P, 1], F32, name="ns8")
        gh = sb.tile([P, PACK], F32, name="gh")
        nc.gpsimd.tensor_tensor(gh[:], gain_sb[:], hsc_sb[:], ALU.mult)

        def interleave(dst, src):
            nc.scalar.copy(
                dst.rearrange("p (c i) t -> p c t i", i=4),
                src.rearrange("p t (c i) -> p c t i", i=4),
            )

        def quantize(codes, scales, src):
            nc.vector.quantize_mx(out=codes.bitcast(FP8X4), scales=scales, in_=src)

        q_bf = sb.tile([P, Q, PACK], BF16, name="q_bf", tag="q_bf", align_bytes=64)
        interleave(q_bf[:], q_raw[:])
        nc.gpsimd.tensor_scalar(ns8[:], sharp_sb[:], -1.0 / GS, 0.0, ALU.mult, ALU.add)
        kwg = sb.tile([P, SLOTS], U16, name="kwg", align_bytes=64)
        ksg = sb.tile([P, SLOTS], U8, name="ksg", align_bytes=64)
        nc.vector.tensor_copy(kwg[:], kw[:].indirect(offsets[:]))
        nc.vector.tensor_copy(ksg[:], ks[:].indirect(offsets[:]))
        q_codes = sb.tile([P, Q], U32, name="q_codes", align_bytes=64)
        q_scales = sb.tile([P, Q], U8, name="q_scales", align_bytes=64)
        quantize(q_codes[:], q_scales[:], q_bf[:].rearrange("p q t -> p (q t)"))
        a_ps = ps.tile([P, SLOTS], F32, name="a_ps")
        nc.tensor.matmul_mx(
            out=a_ps[:], lhsT=q_codes[:].bitcast(FP8X4), lhsT_scale=q_scales[:],
            rhs=kwg[:].bitcast(FP4X4), rhs_scale=ksg[:], start=True, stop=True,
        )
        twg = sb.tile([P, SLOTS], U16, name="twg", tag="q_bf", align_bytes=64)
        tsg = sb.tile([P, SLOTS], U8, name="tsg", align_bytes=64)
        nc.vector.tensor_copy(twg[:], tw[:].indirect(offsets[:]))

        asum = sb.tile([P, G], F32, name="asum", tag="tw")
        nc.vector.tensor_reduce(asum[:], a_ps[:].rearrange("p (g j) -> p g j", j=GS), AX.X, ALU.add)
        nc.vector.tensor_copy(tsg[:], tsc[:].indirect(offsets[:]))

        w_bf = sb.tile([P, PACK, P, PACK], BF16, name="w_bf", tag="w_bf", align_bytes=64)
        def deal(copy, h, m0, m1):
            copy(
                w_bf[:, :, h * 64 + m0 : h * 64 + m1, :].rearrange("p t m j -> p m j t"),
                w_raw[h][:, :, PACK * m0 : PACK * m1].rearrange("p j (m t) -> p m j t", t=PACK),
            )

        deal(nc.scalar.copy, 0, 0, 64)
        deal(nc.scalar.copy, 1, 0, 32)
        deal(nc.vector.tensor_copy, 1, 32, 64)
        p_sb = sb.tile([P, SLOTS], F32, name="p_sb", tag="w_raw1")
        nc.scalar.activation(p_sb[:], a_ps[:], ACT.Exp)
        w_codes = sb.tile([P, R], U32, name="w_codes", align_bytes=64)
        w_scales = sb.tile([P, R], U8, name="w_scales", align_bytes=64)
        quantize(w_codes[:], w_scales[:], w_bf[:].rearrange("p t m j -> p (t m j)"))
        stats = sb.tile([P, 2, G], F32, name="stats", tag="w_bf", align_bytes=64)
        s_sum, nms = stats[:, 0, :], stats[:, 1, :]
        nc.vector.tensor_reduce(s_sum, p_sb[:].rearrange("p (g j) -> p g j", j=GS), AX.X, ALU.add)
        negmax = sb.tile([P, 1], F32, name="negmax")
        nc.vector.tensor_scalar(nms, asum[:], ns8[:], None, ALU.mult, ALU.min, accum_out=negmax[:])
        rs = sb.tile([P, G], F32, name="rs")
        nc.vector.reciprocal(rs[:], s_sum)
        pg = sb.tile([P, G], F32, name="pg")
        z = sb.tile([P, 1], F32, name="z")
        nc.scalar.activation(pg[:], nms, ACT.Exp, bias=negmax[:], scale=-1.0, accum_out=z[:])

        def by_group(ap):
            return ap.rearrange("p (g j) -> p g j", j=GS)

        def spread(ap, groups):
            return ap.unsqueeze(2).to_broadcast([P, groups, GS])

        zh = [ps.tile([P, PACK, CH], F32, name=f"zh{c}") for c in range(NCH)]
        ht = [sb.tile([P, CH, PACK], F32, name=f"ht{c}", tag=f"ht{c}") for c in range(NCH)]
        wide = [CH + Q] + [CH] * (NCH - 1)
        hs = [sb.tile([P, wide[c], PACK], BF16, name=f"hs{c}", align_bytes=64) for c in range(NCH)]
        h_codes = [sb.tile([P, wide[c]], U32, name=f"h_codes{c}", align_bytes=64) for c in range(NCH)]
        h_scales = [sb.tile([P, wide[c]], U8, name=f"h_scales{c}", align_bytes=64) for c in range(NCH)]
        interleave(hs[0][:, CH:, :], g_raw[:])
        FIRST = 3 * CH
        c0a = ps.tile([P, FIRST], F32, name="c0a")
        c0b = ps.tile([P, SLOTS - FIRST], F32, name="c0b")
        c0 = [c0a[:, c * CH : (c + 1) * CH] for c in range(3)] + [c0b[:]]
        for c in range(NCH):
            cols = slice(c * CH, (c + 1) * CH)
            for t in range(PACK):
                m = slice(t * P, (t + 1) * P)
                nc.tensor.matmul_mx(
                    out=zh[c][:, t, :], lhsT=w_codes[:, m].bitcast(FP8X4), lhsT_scale=w_scales[:, m],
                    rhs=twg[:, cols].bitcast(FP4X4), rhs_scale=tsg[:, cols], start=True, stop=True,
                )
            nc.scalar.activation(ht[c][:], zh[c][:].rearrange("p t n -> p n t"), ACT.Tanh)

        def scale_chunk(c):
            nc.vector.tensor_tensor(hs[c][:, :CH, :], ht[c][:], gh[:].unsqueeze(1).to_broadcast([P, CH, PACK]), ALU.mult)

        def product(c):
            quantize(h_codes[c][:], h_scales[c][:], hs[c][:].rearrange("p n t -> p (n t)"))
            nc.tensor.matmul_mx(
                out=c0[c], lhsT=h_codes[0][:, CH:].bitcast(FP8X4), lhsT_scale=h_scales[0][:, CH:],
                rhs=h_codes[c][:, :CH].bitcast(FP8X4), rhs_scale=h_scales[c][:, :CH], start=True, stop=True,
            )

        t_sb = sb.tile([P, SLOTS], F32, name="t_sb")
        u = sb.tile([P, G], F32, name="u")
        x_sb = sb.tile([P, SLOTS], F32, name="x_sb")
        pa, pb = slice(0, FIRST), slice(FIRST, SLOTS)
        ga, gb = slice(0, FIRST // GS), slice(FIRST // GS, G)

        scale_chunk(0)
        n_sb = sb.tile([P, SLOTS], F32, name="n_sb")
        nc.vector.scalar_tensor_tensor(
            by_group(n_sb[:]), by_group(p_sb[:]), 512.0, spread(rs[:], G), ALU.mult, ALU.mult
        )
        rz = sb.tile([P, 1], F32, name="rz")
        nc.vector.reciprocal(rz[:], z[:])
        scale_chunk(1)
        na = sb.tile([P, SLOTS], F32, name="na", tag="ht1")
        nc.scalar.activation(na[:], n_sb[:], ACT.Identity, bias=ns8[:], scale=1.0 / 512.0)
        wb = sb.tile([P, SLOTS], F32, name="wb", tag="ht0")
        nc.scalar.activation(by_group(wb[:]), spread(pg[:], G), ACT.Copy, scale=rz[:])

        product(0)
        scale_chunk(2)
        product(1)
        scale_chunk(3)
        product(2)
        product(3)
        nc.vector.tensor_tensor(t_sb[:, pa], c0a[:], n_sb[:, pa], ALU.mult)
        nc.vector.tensor_tensor(t_sb[:, pb], c0b[:], n_sb[:, pb], ALU.mult)
        nc.vector.tensor_reduce(u[:, ga], by_group(t_sb[:, pa]), AX.X, ALU.add)
        nc.vector.tensor_reduce(u[:, gb], by_group(t_sb[:, pb]), AX.X, ALU.add)
        nc.vector.tensor_tensor(by_group(x_sb[:, pa]), by_group(na[:, pa]), spread(u[:, ga], FIRST // GS), ALU.mult)
        uw = sb.tile([P, G], F32, name="uw")
        negsm = sb.tile([P, 1], F32, name="negsm")
        nc.vector.scalar_tensor_tensor(uw[:], u[:], ns8[:], wb[:, 0:SLOTS:GS], ALU.mult, ALU.mult, accum_out=negsm[:])
        nc.vector.tensor_tensor(by_group(x_sb[:, pb]), by_group(na[:, pb]), spread(u[:, gb], G - FIRST // GS), ALU.mult)
        y_sb = sb.tile([P, SLOTS], F32, name="y_sb")
        nc.vector.scalar_tensor_tensor(y_sb[:], t_sb[:], negsm[:], x_sb[:], ALU.add, ALU.subtract)
        nc.vector.tensor_tensor(window[:].indirect(offsets[:]), y_sb[:], wb[:], ALU.mult)

        bounds = [0, 256, 768, 1280, 1792, 2048]
        for k in range(len(bounds) - 1):
            cols = slice(bounds[k], bounds[k + 1])
            res = sb.tile([P, bounds[k + 1] - bounds[k]], F32, name=f"res{k}")
            nc.vector.tensor_tensor(res[:], window[:, cols], old_sb[:, cols], ALU.add)
            (nc.sync if k % 2 == 0 else nc.scalar).dma_start(out[:, cols], res[:])
